import numpy as np, ml_dtypes
CORES = [32,160,288,416,80,208,336,464]
N = 8
GR, GC, HH, WW = 2, 4, 16, 16
def setup_inputs(rng):
    return {"x": rng.standard_normal((N, 128, HH * WW), dtype=np.float32).astype(ml_dtypes.bfloat16), "w": rng.standard_normal((N, 128, 9 * 128), dtype=np.float32).astype(ml_dtypes.bfloat16)}
def setup_inputs_big(rng):
    d = setup_inputs(rng)
    for k in ("x", "w"): d[k] = (d[k].astype(np.float32) * 1024.0).astype(d[k].dtype)
    return d
def setup_inputs_small(rng):
    d = setup_inputs(rng)
    for k in ("x", "w"): d[k] = (d[k].astype(np.float32) * (1 / 1024.0)).astype(d[k].dtype)
    return d
def setup_inputs_apart(rng):
    d = setup_inputs(rng)
    f = (10.0 ** rng.permutation(np.linspace(-1.5, 1.5, N))).astype(np.float32).reshape(N, 1, 1)
    for k in ("x", "w"): d[k] = (d[k].astype(np.float32) * f).astype(d[k].dtype)
    return d
def reference(x, w):
    X = x.astype(np.float64).reshape(GR, GC, 128, HH, WW); W = w.astype(np.float64)
    g = np.concatenate([np.concatenate(list(X[i]), axis=2) for i in range(GR)], axis=1)
    y = np.zeros((N, 128, HH * WW))
    for r in range(N):
        i0, j0 = HH * (r // GC), WW * (r % GC)
        for a in range(3):
            for b in range(3):
                sh = np.roll(g, (-2 * (a - 1), -2 * (b - 1)), axis=(1, 2))[:, i0:i0 + HH, j0:j0 + WW]
                y[r] += W[r][:, 128 * (3 * a + b):128 * (3 * a + b) + 128].T @ sh.reshape(128, HH * WW)
    return {"y": y.astype(ml_dtypes.bfloat16 if x.dtype != np.float64 else np.float64)}

@@ -1,0 +1,111 @@
+from concourse.bass import DstId, RemoteDMATransfer
+
+GR, GC, HH, WW = 2, 4, 16, 16
+D = 2
+
+SCRATCH = {
+    "xs": ("sbuf", [128, HH, WW], "bfloat16"),
+    "ws": ("sbuf", [128, 9 * 128], "bfloat16"),
+    "pl": ("sbuf", [128, HH, D], "bfloat16"),
+    "pr": ("sbuf", [128, HH, D], "bfloat16"),
+    "ht": ("sbuf", [128, D, WW], "bfloat16"),
+    "hb": ("sbuf", [128, D, WW], "bfloat16"),
+    "sl": ("sbuf", [128, 2 * HH, D], "bfloat16"),
+    "sr": ("sbuf", [128, 2 * HH, D], "bfloat16"),
+    "ps": ("psum", [128, HH, WW], "float32"),
+    "ys": ("sbuf", [128, HH, WW], "bfloat16"),
+}
+SEMAPHORES = ["xl", "wl", "pk", "sent", "sv", "sla", "sra", "mm", "cp", "st"]
+
+
+def own(t, n):
+    return max(0, D - D * t), min(n, n + D - D * t)
+
+
+def rank_program(g, core, T, topo):
+    rank = T.rank_of(core)
+    if rank is None:
+        return
+    S = T.sem
+    gr, gc = rank // GC, rank % GC
+
+    def at(r, c):
+        return T.cores[(r % GR) * GC + (c % GC)]
+
+    V, L, R = at(gr + 1, gc), at(gr, gc - 1), at(gr, gc + 1)
+    VL, VR = at(gr + 1, gc - 1), at(gr + 1, gc + 1)
+
+    m = topo.mask(core, V)
+    for d in (L, R, VL, VR):
+        m &= topo.mask(core, d)
+    eng = [e for e in range(16) if (m >> e) & 1]
+    ne = len(eng)
+
+    def xfer(dst_core, dst, src, es, sem):
+        rid, pid = topo.addr(dst_core, core)
+        return RemoteDMATransfer(dst_ids=[DstId(rid=rid, pnc=pid)], dma_engine_mask=sum(1 << e for e in es),
+                                 remote_sem=sem, src=src, dst=dst)
+
+    g.sync.dma_start(T.xs[:], T.x[:]).then_inc(S.xl, 16)
+    g.sync.dma_start(T.ws[:], T.w[:]).then_inc(S.wl, 16)
+
+    v = g.vector
+    v.wait_ge(S.xl, 16)
+    v.tensor_copy(T.pl[:], T.xs[:, :, 0:D]).then_inc(S.pk, 1)
+    v.tensor_copy(T.pr[:], T.xs[:, :, WW - D:WW]).then_inc(S.pk, 1)
+
+    g.wait_ge(S.xl, 16)
+    h = ne // 2
+    g.remote_dma_fused([
+        xfer(V, T.hb[:], T.xs[:, 0:D, :], eng[:h], S.sv),
+        xfer(V, T.ht[:], T.xs[:, HH - D:HH, :], eng[h:], S.sv),
+    ], local_sem=S.sent)
+    g.wait_ge(S.pk, 2)
+    q = ne // 4
+    g.remote_dma_fused([
+        xfer(L, T.sr[:, 0:HH, :], T.pl[:], eng[0:q], S.sra),
+        xfer(VL, T.sr[:, HH:2 * HH, :], T.pl[:], eng[q:2 * q], S.sra),
+        xfer(R, T.sl[:, 0:HH, :], T.pr[:], eng[2 * q:3 * q], S.sla),
+        xfer(VR, T.sl[:, HH:2 * HH, :], T.pr[:], eng[3 * q:4 * q], S.sla),
+    ], local_sem=S.sent)
+
+    def W(a, b):
+        k = 128 * (3 * a + b)
+        return T.ws[:, k:k + 128]
+
+    mms = []
+    taps = [(1, 1)] + [(a, b) for a in range(3) for b in range(3) if (a, b) != (1, 1)]
+    for a, b in taps:
+        i0, i1 = own(a, HH)
+        j0, j1 = own(b, WW)
+        di, dj = D * (a - 1), D * (b - 1)
+        mms.append((None, T.ps[:, i0:i1, j0:j1], (a, b), T.xs[:, i0 + di:i1 + di, j0 + dj:j1 + dj]))
+    first = (S.sv, 2 * h)
+    for b in range(3):
+        j0, j1 = own(b, WW)
+        dj = D * (b - 1)
+        mms.append((first, T.ps[:, 0:D, j0:j1], (0, b), T.ht[:, :, j0 + dj:j1 + dj]))
+        first = None
+        mms.append((None, T.ps[:, HH - D:HH, j0:j1], (2, b), T.hb[:, :, j0 + dj:j1 + dj]))
+    strips = [(0, T.sl, 0, S.sla, L), (2, T.sr, WW - D, S.sra, R)]
+    strips.sort(key=lambda s: topo.rack(topo.host(s[4])) != topo.rack(topo.host(core)))
+    for b, s, c0, sem, _ in strips:
+        mms.append(((sem, 2 * q), T.ps[:, D:HH, c0:c0 + D], (0, b), s[:, 0:HH - D, :]))
+        mms.append((None, T.ps[:, 0:D, c0:c0 + D], (0, b), s[:, 2 * HH - D:2 * HH, :]))
+        mms.append((None, T.ps[:, :, c0:c0 + D], (1, b), s[:, 0:HH, :]))
+        mms.append((None, T.ps[:, :, c0:c0 + D], (2, b), s[:, D:HH + D, :]))
+
+    t = g.tensor
+    t.wait_ge(S.xl, 16)
+    t.wait_ge(S.wl, 16)
+    for k, (wait, out, (a, b), rhs) in enumerate(mms):
+        if wait is not None:
+            t.wait_ge(wait[0], wait[1])
+        t.matmul(out, W(a, b), rhs, k == 0, k == len(mms) - 1).then_inc(S.mm, 1)
+
+    v.wait_ge(S.mm, len(mms))
+    v.tensor_copy(T.ys[:], T.ps[:]).then_inc(S.cp, 1)
+    g.sync.wait_ge(S.cp, 1)
+    g.sync.dma_start(T.y[:], T.ys[:]).then_inc(S.st, 16)
+    g.sync.wait_ge(S.st, 16)
+    g.wait_ge(S.sent, 2 * h + 4 * q)

@@ -1,21 +1,27 @@
 from concourse.bass import DstId, RemoteDMATransfer
+from concourse.mybir import AluOpType
 
 GR, GC, HH, WW = 2, 4, 16, 16
 D = 2
 
 SCRATCH = {
-    "xs": ("sbuf", [128, HH, WW], "bfloat16"),
+    "xs": ("sbuf", [128, D + HH, WW], "bfloat16"),
     "ws": ("sbuf", [128, 9 * 128], "bfloat16"),
-    "pl": ("sbuf", [128, HH, D], "bfloat16"),
-    "pr": ("sbuf", [128, HH, D], "bfloat16"),
-    "ht": ("sbuf", [128, D, WW], "bfloat16"),
-    "hb": ("sbuf", [128, D, WW], "bfloat16"),
-    "sl": ("sbuf", [128, 2 * HH, D], "bfloat16"),
-    "sr": ("sbuf", [128, 2 * HH, D], "bfloat16"),
-    "ps": ("psum", [128, HH, WW], "float32"),
+    "pl": ("sbuf", [128, D + HH, D], "bfloat16"),
+    "pr": ("sbuf", [128, D + HH, D], "bfloat16"),
+    "hv": ("sbuf", [128, 2 * D, WW], "bfloat16"),
+    "sl": ("sbuf", [128, HH, D], "bfloat16"),
+    "sr": ("sbuf", [128, HH, D], "bfloat16"),
+    "cl": ("sbuf", [128, 2 * D, D], "bfloat16"),
+    "cr": ("sbuf", [128, 2 * D, D], "bfloat16"),
+    "pa": ("psum", [128, 2 * HH, WW], "float32"),
+    "pbl": ("psum", [128, 2 * HH, WW], "float32"),
+    "pbr": ("psum", [128, 2 * HH, WW], "float32"),
+    "ael": ("sbuf", [128, HH, D], "float32"),
+    "aer": ("sbuf", [128, HH, D], "float32"),
     "ys": ("sbuf", [128, HH, WW], "bfloat16"),
 }
-SEMAPHORES = ["xl", "wl", "pk", "sent", "sv", "sla", "sra", "mm", "cp", "st"]
+SEMAPHORES = ["xl", "w0", "w1", "w2", "pk", "sent", "sv", "sla", "sra", "cla", "cra", "ma", "ml", "mr", "vc", "fin", "st"]
 
 
 def own(t, n):
@@ -40,72 +46,85 @@ def rank_program(g, core, T, topo):
         m &= topo.mask(core, d)
     eng = [e for e in range(16) if (m >> e) & 1]
     ne = len(eng)
+    h = ne // 2
 
     def xfer(dst_core, dst, src, es, sem):
         rid, pid = topo.addr(dst_core, core)
         return RemoteDMATransfer(dst_ids=[DstId(rid=rid, pnc=pid)], dma_engine_mask=sum(1 << e for e in es),
                                  remote_sem=sem, src=src, dst=dst)
 
-    g.sync.dma_start(T.xs[:], T.x[:]).then_inc(S.xl, 16)
-    g.sync.dma_start(T.ws[:], T.w[:]).then_inc(S.wl, 16)
+    g.sync.dma_start(T.xs[:, D:D + HH, :], T.x[:]).then_inc(S.xl, 16)
+    g.scalar.dma_start(T.xs[:, 0:D, :], T.x[:, (HH - D) * WW:HH * WW]).then_inc(S.xl, 16)
+    XL = 32
+    wsem = [S.w0, S.w1, S.w2]
+    arow = [1, 0, 2]
+    for a in arow:
+        g.scalar.dma_start(T.ws[:, 384 * a:384 * (a + 1)], T.w[:, 384 * a:384 * (a + 1)]).then_inc(wsem[a], 16)
 
     v = g.vector
-    v.wait_ge(S.xl, 16)
+    v.wait_ge(S.xl, XL)
     v.tensor_copy(T.pl[:], T.xs[:, :, 0:D]).then_inc(S.pk, 1)
     v.tensor_copy(T.pr[:], T.xs[:, :, WW - D:WW]).then_inc(S.pk, 1)
 
-    g.wait_ge(S.xl, 16)
-    h = ne // 2
-    g.remote_dma_fused([
-        xfer(V, T.hb[:], T.xs[:, 0:D, :], eng[:h], S.sv),
-        xfer(V, T.ht[:], T.xs[:, HH - D:HH, :], eng[h:], S.sv),
-    ], local_sem=S.sent)
+    g.wait_ge(S.xl, XL)
+    g.remote_dma_fused([xfer(V, T.hv[:], T.xs[:, 0:2 * D, :], eng, S.sv)], local_sem=S.sent)
     g.wait_ge(S.pk, 2)
-    q = ne // 4
     g.remote_dma_fused([
-        xfer(L, T.sr[:, 0:HH, :], T.pl[:], eng[0:q], S.sra),
-        xfer(VL, T.sr[:, HH:2 * HH, :], T.pl[:], eng[q:2 * q], S.sra),
-        xfer(R, T.sl[:, 0:HH, :], T.pr[:], eng[2 * q:3 * q], S.sla),
-        xfer(VR, T.sl[:, HH:2 * HH, :], T.pr[:], eng[3 * q:4 * q], S.sla),
+        xfer(L, T.sr[:], T.pl[:, D:D + HH, :], eng[:h], S.sra),
+        xfer(R, T.sl[:], T.pr[:, D:D + HH, :], eng[h:], S.sla),
+    ], local_sem=S.sent)
+    g.remote_dma_fused([
+        xfer(VL, T.cr[:], T.pl[:, 0:2 * D, :], eng[:h], S.cra),
+        xfer(VR, T.cl[:], T.pr[:, 0:2 * D, :], eng[h:], S.cla),
     ], local_sem=S.sent)
 
     def W(a, b):
         k = 128 * (3 * a + b)
         return T.ws[:, k:k + 128]
 
-    mms = []
-    taps = [(1, 1)] + [(a, b) for a in range(3) for b in range(3) if (a, b) != (1, 1)]
-    for a, b in taps:
-        i0, i1 = own(a, HH)
-        j0, j1 = own(b, WW)
-        di, dj = D * (a - 1), D * (b - 1)
-        mms.append((None, T.ps[:, i0:i1, j0:j1], (a, b), T.xs[:, i0 + di:i1 + di, j0 + dj:j1 + dj]))
-    first = (S.sv, 2 * h)
+    t = g.tensor
+    t.wait_ge(S.xl, XL)
+    na = 9 + 6
+    k = 0
+    for a in arow:
+        t.wait_ge(wsem[a], 16)
+        for b in (1, 0, 2):
+            i0, i1 = own(a, HH)
+            j0, j1 = own(b, WW)
+            di, dj = D * (a - 1) + D, D * (b - 1)
+            t.matmul(T.pa[:, i0:i1, j0:j1], W(a, b), T.xs[:, i0 + di:i1 + di, j0 + dj:j1 + dj],
+                     k == 0, False).then_inc(S.ma, 1)
+            k += 1
+    t.wait_ge(S.sv, ne)
     for b in range(3):
         j0, j1 = own(b, WW)
         dj = D * (b - 1)
-        mms.append((first, T.ps[:, 0:D, j0:j1], (0, b), T.ht[:, :, j0 + dj:j1 + dj]))
-        first = None
-        mms.append((None, T.ps[:, HH - D:HH, j0:j1], (2, b), T.hb[:, :, j0 + dj:j1 + dj]))
-    strips = [(0, T.sl, 0, S.sla, L), (2, T.sr, WW - D, S.sra, R)]
-    strips.sort(key=lambda s: topo.rack(topo.host(s[4])) != topo.rack(topo.host(core)))
-    for b, s, c0, sem, _ in strips:
-        mms.append(((sem, 2 * q), T.ps[:, D:HH, c0:c0 + D], (0, b), s[:, 0:HH - D, :]))
-        mms.append((None, T.ps[:, 0:D, c0:c0 + D], (0, b), s[:, 2 * HH - D:2 * HH, :]))
-        mms.append((None, T.ps[:, :, c0:c0 + D], (1, b), s[:, 0:HH, :]))
-        mms.append((None, T.ps[:, :, c0:c0 + D], (2, b), s[:, D:HH + D, :]))
+        t.matmul(T.pa[:, 0:D, j0:j1], W(0, b), T.hv[:, 0:D, j0 + dj:j1 + dj], False, False).then_inc(S.ma, 1)
+        t.matmul(T.pa[:, HH - D:HH, j0:j1], W(2, b), T.hv[:, D:2 * D, j0 + dj:j1 + dj], False, b == 2).then_inc(S.ma, 1)
 
-    t = g.tensor
-    t.wait_ge(S.xl, 16)
-    t.wait_ge(S.wl, 16)
-    for k, (wait, out, (a, b), rhs) in enumerate(mms):
-        if wait is not None:
-            t.wait_ge(wait[0], wait[1])
-        t.matmul(out, W(a, b), rhs, k == 0, k == len(mms) - 1).then_inc(S.mm, 1)
+    sides = [(0, T.sl, T.cl, S.sla, S.cla, T.pbl, S.ml, T.ael, 0, L),
+             (2, T.sr, T.cr, S.sra, S.cra, T.pbr, S.mr, T.aer, WW - D, R)]
+    sides.sort(key=lambda s: topo.rack(topo.host(s[9])) != topo.rack(topo.host(core)))
+    for b, s, c, ssem, csem, pb, msem, ae, c0, _ in sides:
+        t.wait_ge(ssem, h)
+        t.matmul(pb[:, 0:HH, 0:D], W(1, b), s[:], True, False).then_inc(msem, 1)
+        t.matmul(pb[:, D:HH, 0:D], W(0, b), s[:, 0:HH - D, :], False, False).then_inc(msem, 1)
+        t.matmul(pb[:, 0:HH - D, 0:D], W(2, b), s[:, D:HH, :], False, False).then_inc(msem, 1)
+    for b, s, c, ssem, csem, pb, msem, ae, c0, _ in sides:
+        t.wait_ge(csem, h)
+        t.matmul(pb[:, 0:D, 0:D], W(0, b), c[:, 0:D, :], False, False).then_inc(msem, 1)
+        t.matmul(pb[:, HH - D:HH, 0:D], W(2, b), c[:, D:2 * D, :], False, True).then_inc(msem, 1)
 
-    v.wait_ge(S.mm, len(mms))
-    v.tensor_copy(T.ys[:], T.ps[:]).then_inc(S.cp, 1)
-    g.sync.wait_ge(S.cp, 1)
+    v.wait_ge(S.ma, na)
+    v.tensor_copy(T.ael[:], T.pa[:, 0:HH, 0:D]).then_inc(S.vc, 1)
+    v.tensor_copy(T.aer[:], T.pa[:, 0:HH, WW - D:WW]).then_inc(S.vc, 1)
+    v.tensor_copy(T.ys[:, :, D:WW - D], T.pa[:, 0:HH, D:WW - D]).then_inc(S.fin, 1)
+    v.wait_ge(S.vc, 2)
+    for b, s, c, ssem, csem, pb, msem, ae, c0, _ in sides:
+        v.wait_ge(msem, 5)
+        v.tensor_tensor(T.ys[:, :, c0:c0 + D], ae[:], pb[:, 0:HH, 0:D], AluOpType.add).then_inc(S.fin, 1)
+
+    g.sync.wait_ge(S.fin, 3)
     g.sync.dma_start(T.y[:], T.ys[:]).then_inc(S.st, 16)
     g.sync.wait_ge(S.st, 16)
-    g.wait_ge(S.sent, 2 * h + 4 * q)
+    g.wait_ge(S.sent, ne + 4 * h)

from concourse.bass import DstId, RemoteDMATransfer
from concourse.mybir import AluOpType

GR, GC, HH, WW = 2, 4, 16, 16
D = 2

SCRATCH = {
    "xs": ("sbuf", [128, D + HH, WW], "bfloat16"),
    "ws": ("sbuf", [128, 9 * 128], "bfloat16"),
    "pl": ("sbuf", [128, D + HH, D], "bfloat16"),
    "pr": ("sbuf", [128, D + HH, D], "bfloat16"),
    "hv": ("sbuf", [128, 2 * D, WW], "bfloat16"),
    "sl": ("sbuf", [128, HH, D], "bfloat16"),
    "sr": ("sbuf", [128, HH, D], "bfloat16"),
    "cl": ("sbuf", [128, 2 * D, D], "bfloat16"),
    "cr": ("sbuf", [128, 2 * D, D], "bfloat16"),
    "pa": ("psum", [128, 2 * HH, WW], "float32"),
    "pbl": ("psum", [128, 2 * HH, WW], "float32"),
    "pbr": ("psum", [128, 2 * HH, WW], "float32"),
    "ael": ("sbuf", [128, HH, D], "float32"),
    "aer": ("sbuf", [128, HH, D], "float32"),
    "ys": ("sbuf", [128, HH, WW], "bfloat16"),
}
SEMAPHORES = ["xl", "w0", "w1", "w2", "pk", "sent", "sv", "sla", "sra", "cla", "cra", "ma", "ml", "mr", "vc", "fin", "st"]


def own(t, n):
    return max(0, D - D * t), min(n, n + D - D * t)


def rank_program(g, core, T, topo):
    rank = T.rank_of(core)
    if rank is None:
        return
    S = T.sem
    gr, gc = rank // GC, rank % GC

    def at(r, c):
        return T.cores[(r % GR) * GC + (c % GC)]

    V, L, R = at(gr + 1, gc), at(gr, gc - 1), at(gr, gc + 1)
    VL, VR = at(gr + 1, gc - 1), at(gr + 1, gc + 1)

    m = topo.mask(core, V)
    for d in (L, R, VL, VR):
        m &= topo.mask(core, d)
    eng = [e for e in range(16) if (m >> e) & 1]
    ne = len(eng)
    h = ne // 2

    def xfer(dst_core, dst, src, es, sem):
        rid, pid = topo.addr(dst_core, core)
        return RemoteDMATransfer(dst_ids=[DstId(rid=rid, pnc=pid)], dma_engine_mask=sum(1 << e for e in es),
                                 remote_sem=sem, src=src, dst=dst)

    g.sync.dma_start(T.xs[:, D:D + HH, :], T.x[:]).then_inc(S.xl, 16)
    g.scalar.dma_start(T.xs[:, 0:D, :], T.x[:, (HH - D) * WW:HH * WW]).then_inc(S.xl, 16)
    XL = 32
    wsem = [S.w0, S.w1, S.w2]
    arow = [1, 0, 2]
    for a in arow:
        g.scalar.dma_start(T.ws[:, 384 * a:384 * (a + 1)], T.w[:, 384 * a:384 * (a + 1)]).then_inc(wsem[a], 16)

    v = g.vector
    v.wait_ge(S.xl, XL)
    v.tensor_copy(T.pl[:], T.xs[:, :, 0:D]).then_inc(S.pk, 1)
    v.tensor_copy(T.pr[:], T.xs[:, :, WW - D:WW]).then_inc(S.pk, 1)

    g.wait_ge(S.xl, XL)
    g.remote_dma_fused([xfer(V, T.hv[:], T.xs[:, 0:2 * D, :], eng, S.sv)], local_sem=S.sent)
    g.wait_ge(S.pk, 2)
    g.remote_dma_fused([
        xfer(L, T.sr[:], T.pl[:, D:D + HH, :], eng[:h], S.sra),
        xfer(R, T.sl[:], T.pr[:, D:D + HH, :], eng[h:], S.sla),
    ], local_sem=S.sent)
    g.remote_dma_fused([
        xfer(VL, T.cr[:], T.pl[:, 0:2 * D, :], eng[:h], S.cra),
        xfer(VR, T.cl[:], T.pr[:, 0:2 * D, :], eng[h:], S.cla),
    ], local_sem=S.sent)

    def W(a, b):
        k = 128 * (3 * a + b)
        return T.ws[:, k:k + 128]

    t = g.tensor
    t.wait_ge(S.xl, XL)
    na = 9 + 6
    k = 0
    for a in arow:
        t.wait_ge(wsem[a], 16)
        for b in (1, 0, 2):
            i0, i1 = own(a, HH)
            j0, j1 = own(b, WW)
            di, dj = D * (a - 1) + D, D * (b - 1)
            t.matmul(T.pa[:, i0:i1, j0:j1], W(a, b), T.xs[:, i0 + di:i1 + di, j0 + dj:j1 + dj],
                     k == 0, False).then_inc(S.ma, 1)
            k += 1
    t.wait_ge(S.sv, ne)
    for b in range(3):
        j0, j1 = own(b, WW)
        dj = D * (b - 1)
        t.matmul(T.pa[:, 0:D, j0:j1], W(0, b), T.hv[:, 0:D, j0 + dj:j1 + dj], False, False).then_inc(S.ma, 1)
        t.matmul(T.pa[:, HH - D:HH, j0:j1], W(2, b), T.hv[:, D:2 * D, j0 + dj:j1 + dj], False, b == 2).then_inc(S.ma, 1)

    sides = [(0, T.sl, T.cl, S.sla, S.cla, T.pbl, S.ml, T.ael, 0, L),
             (2, T.sr, T.cr, S.sra, S.cra, T.pbr, S.mr, T.aer, WW - D, R)]
    sides.sort(key=lambda s: topo.rack(topo.host(s[9])) != topo.rack(topo.host(core)))
    for b, s, c, ssem, csem, pb, msem, ae, c0, _ in sides:
        t.wait_ge(ssem, h)
        t.matmul(pb[:, 0:HH, 0:D], W(1, b), s[:], True, False).then_inc(msem, 1)
        t.matmul(pb[:, D:HH, 0:D], W(0, b), s[:, 0:HH - D, :], False, False).then_inc(msem, 1)
        t.matmul(pb[:, 0:HH - D, 0:D], W(2, b), s[:, D:HH, :], False, False).then_inc(msem, 1)
    for b, s, c, ssem, csem, pb, msem, ae, c0, _ in sides:
        t.wait_ge(csem, h)
        t.matmul(pb[:, 0:D, 0:D], W(0, b), c[:, 0:D, :], False, False).then_inc(msem, 1)
        t.matmul(pb[:, HH - D:HH, 0:D], W(2, b), c[:, D:2 * D, :], False, True).then_inc(msem, 1)

    v.wait_ge(S.ma, na)
    v.tensor_copy(T.ael[:], T.pa[:, 0:HH, 0:D]).then_inc(S.vc, 1)
    v.tensor_copy(T.aer[:], T.pa[:, 0:HH, WW - D:WW]).then_inc(S.vc, 1)
    v.tensor_copy(T.ys[:, :, D:WW - D], T.pa[:, 0:HH, D:WW - D]).then_inc(S.fin, 1)
    v.wait_ge(S.vc, 2)
    for b, s, c, ssem, csem, pb, msem, ae, c0, _ in sides:
        v.wait_ge(msem, 5)
        v.tensor_tensor(T.ys[:, :, c0:c0 + D], ae[:], pb[:, 0:HH, 0:D], AluOpType.add).then_inc(S.fin, 1)

    g.sync.wait_ge(S.fin, 3)
    g.sync.dma_start(T.y[:], T.ys[:]).then_inc(S.st, 16)
    g.sync.wait_ge(S.st, 16)
    g.wait_ge(S.sent, ne + 4 * h)
